import numpy as np
import ml_dtypes


def mxq(x, axis, fmt="e4m3"):
    dtype, down = {"e4m3": (ml_dtypes.float8_e4m3fn, 7), "e5m2": (ml_dtypes.float8_e5m2, 14)}[fmt]
    v = np.moveaxis(np.asarray(x, np.float32).astype(ml_dtypes.bfloat16).astype(np.float64), axis, -1)
    blocks = v.reshape(v.shape[:-1] + (-1, 32))
    amax = np.abs(blocks).max(-1, keepdims=True)
    byte = np.maximum(np.where(amax > 0, np.frexp(amax)[1] - 1 + 127, 0) - down, 1)
    scale = np.exp2(byte - 127.0)
    codes = (blocks / scale).astype(np.float32).astype(dtype).astype(np.float64)
    return np.moveaxis((codes * scale).reshape(v.shape), -1, axis)


WIDE = False


def mx_kscale(k):
    if not WIDE:
        return np.ones(k)
    levels = np.array([10, -10, 5, -5, 0])
    if k % 512:
        return np.exp2(np.random.permutation(np.resize(levels, k // 32))).repeat(32)
    a = np.empty((k // 512, 16))
    for p in range(k // 512):
        a[p, :8] = np.random.permutation(np.resize(levels, 8))
        for g in range(8):
            far = levels[np.abs(levels - a[p, g]) >= 10]
            a[p, g + 8] = far[np.random.randint(len(far))]
    return np.exp2(a.ravel()).repeat(32)


def f64(x):
    return np.asarray(x).astype(np.float64)


def striped8(idx):
    return np.asarray(idx).reshape(8, -1, 16).transpose(0, 2, 1).reshape(128, -1).astype(np.uint16)


def unstriped8(offs):
    return offs.reshape(8, 16, -1).transpose(0, 2, 1).reshape(8, -1).astype(np.int64)


def pick8(x, idx, run):
    r = np.arange(len(x))
    return x[r[:, None], idx[r % (8 * run) // run]]


E2M1 = np.array([0.0, 0.5, 1.0, 1.5, 2.0, 3.0, 4.0, 6.0, -0.0, -0.5, -1.0, -1.5, -2.0, -3.0, -4.0, -6.0])


def pack_weight(w, fmt):
    k, n = w.shape
    w = f64(np.asarray(w, np.float32).astype(ml_dtypes.bfloat16)).reshape(k // 32, 32, n)
    amax = np.abs(w).max(1)
    if fmt == "e4m3":
        byte = np.frexp(amax)[1] - 1 + 127 - 7
    else:
        mant, ex = np.frexp(amax / 6.0)
        byte = np.where(mant > 0.5, ex, ex - 1) + 127
    byte = np.clip(np.where(amax > 0, byte, 1), 1, 254)
    scaled = (w * np.exp2(127.0 - byte)[:, None, :]).reshape(k, n).astype(np.float32)
    by_word = np.ascontiguousarray(scaled.reshape(k // 512, 128, 4, n).transpose(0, 1, 3, 2))
    if fmt == "e4m3":
        words = by_word.astype(ml_dtypes.float8_e4m3fn).view(np.uint8)
    else:
        c = by_word.astype(ml_dtypes.float4_e2m1fn).view(np.uint8) & 0xF
        words = (c[..., 0::2] | (c[..., 1::2] << 4)).reshape(k // 512, 128, 2 * n)
    return np.ascontiguousarray(words), np.ascontiguousarray(byte.astype(np.uint8).reshape(k // 512, 16, n))


def unpack_weight(words, scales, fmt):
    g, _, n = scales.shape
    words = np.ascontiguousarray(words).reshape(g, 128, n, -1)
    if fmt == "e4m3":
        vals = words.view(ml_dtypes.float8_e4m3fn).astype(np.float64)
    else:
        nib = np.empty((g, 128, n, 4), np.uint8)
        nib[..., 0::2] = words & 0xF
        nib[..., 1::2] = words >> 4
        vals = E2M1[nib]
    vals = vals * np.repeat(np.exp2(scales.astype(np.float64) - 127.0), 8, axis=1)[..., None]
    return vals.transpose(0, 1, 3, 2).reshape(g * 512, n)


def softplus(v):
    return np.log(1.0 + np.exp(v))


D, T, I, Q = 512, 1024, 512, 128


def setup_inputs():
    n = np.random.standard_normal
    idx = np.stack([np.random.permutation(T)[:I] for _ in range(8)])
    idx2 = np.stack([np.random.permutation(T)[:I] for _ in range(8)])
    idx3 = np.stack([np.random.permutation(T)[:I] for _ in range(8)])
    fd = mx_kscale(D)
    keysp = pack_weight(n((D, T)) / fd[:, None], "e2m1")
    return {
        "query": (n((D, Q)) * 0.9 / np.sqrt(D) * fd[:, None]).astype(np.float32),
        "query2": (n((D, Q)) * 0.9 / np.sqrt(D) * fd[:, None]).astype(np.float32),
        "keys_words": keysp[0],
        "keys_scales": keysp[1],
        "lam": (np.random.uniform(0.6, 1.2, (Q, 1))).astype(np.float32),
        "old": (1.0 * n((Q, T))).astype(np.float32),
        "offs": striped8(idx),
        "offs2": striped8(idx2),
        "offs3": striped8(idx3),
    }


def reference(query, query2, keys_words, keys_scales, lam, old, offs, offs2, offs3):
    idx = unstriped8(offs)
    idx2 = unstriped8(offs2)
    idx3 = unstriped8(offs3)
    keysu = unpack_weight(keys_words, keys_scales, "e2m1")
    queryq = mxq(f64(query), 0, "e4m3")
    a = queryq.T @ keysu
    query2q = mxq(f64(query2), 0, "e4m3")
    b = query2q.T @ keysu
    w = pick8(a, idx, 16) / (softplus(pick8(b, idx2, 16)) + 0.5) * f64(lam)
    f1 = np.zeros((Q, T))
    f1[np.arange(Q)[:, None], idx[np.arange(Q) % 128 // 16]] = w
    f2 = f1 + f64(old)
    y = pick8(f2, idx3, 16)
    return y

@@ -1,0 +1,174 @@
+import math
+from contextlib import ExitStack
+
+import concourse.mybir as mybir
+
+D, T, I, Q = 512, 1024, 512, 128
+FLOPS = 2 * 2 * D * T * Q
+
+F32 = mybir.dt.float32
+BF16 = mybir.dt.bfloat16
+I32 = mybir.dt.int32
+U32 = mybir.dt.uint32
+U16 = mybir.dt.uint16
+U8 = mybir.dt.uint8
+FP8X4 = mybir.dt.float8_e4m3fn_x4
+FP4X4 = mybir.dt.float4_e2m1fn_x4
+ALU = mybir.AluOpType
+ACT = mybir.ActivationFunctionType
+
+P = 128
+PACK = 4
+LANES = 16
+HALF = I // 2
+FIRST = 128
+TINY = 2.0 ** -63
+
+
+def tile_attend_worthfor_lean_through_heads_kernel(tc, query, query2, keys_words, keys_scales, lam, old, offs, offs2, offs3, out):
+    nc = tc.nc
+    with ExitStack() as ctx:
+        sb = ctx.enter_context(tc.tile_pool(name="sb", bufs=1))
+        ps = ctx.enter_context(tc.psum_pool(name="ps", bufs=1))
+
+        def cols(lo, hi):
+            return slice(lo // LANES, hi // LANES)
+
+        list_a = sb.tile([P, I // LANES], U16, name="list_a")
+        list_b = sb.tile([P, I // LANES], U16, name="list_b")
+        list_o = sb.tile([P, I // LANES], U16, name="list_o")
+
+        key_scales = sb.tile([P, T], U8, name="key_scales", align_bytes=64)
+        nc.vector.memset(key_scales[:].bitcast(I32), 0)
+        lam_col = sb.tile([P, 1], F32, name="lam_col")
+        nc.scalar.dma_start(lam_col[:], lam)
+        zero = sb.tile([P, HALF], F32, name="zero")
+        nc.vector.memset(zero[:], 0.0)
+        half = sb.tile([P, 1], F32, name="half")
+        nc.scalar.activation(half[:], zero[:, 0:1], ACT.Sigmoid)
+        lam_wide = sb.tile([P, HALF], F32, name="lam_wide")
+        nc.scalar.activation(lam_wide[:], zero[:], ACT.Identity, bias=lam_col[:])
+
+        raw_b = sb.tile([P, PACK, Q], F32, name="raw_b")
+        nc.sync.dma_start(raw_b[:], query2.rearrange("(p j) q -> p j q", j=PACK))
+        for quad in range(4):
+            nc.sync.dma_start(
+                key_scales[32 * quad : 32 * quad + 4, :].bitcast(I32),
+                keys_scales[0, 4 * quad : 4 * quad + 4, :].bitcast(I32),
+            )
+        key_words = sb.tile([P, 2 * T], U8, name="key_words", align_bytes=64)
+        nc.sync.dma_start(key_words[:].bitcast(I32), keys_words[0].bitcast(I32))
+        raw_a = sb.tile([P, PACK, Q], F32, name="raw_a")
+        nc.sync.dma_start(raw_a[:], query.rearrange("(p j) q -> p j q", j=PACK))
+        nc.sync.dma_start(list_b[:], offs2)
+        nc.sync.dma_start(list_a[:], offs)
+        totals = sb.tile([P, T], F32, name="totals")
+        nc.sync.dma_start(totals[:], old)
+        nc.sync.dma_start(list_o[:], offs3)
+
+        placed = sb.tile([P, T], F32, name="placed")
+        nc.vector.memset(placed[:], 0.0)
+
+        def views(woven, raw, lo, hi):
+            return (woven[:, lo:hi, :].rearrange("p (c i) j -> p c j i", i=4), raw[:, :, lo:hi].rearrange("p j (c i) -> p c j i", i=4))
+
+        woven_b = sb.tile([P, Q, PACK], BF16, name="woven_b", align_bytes=64)
+        woven_a = sb.tile([P, Q, PACK], BF16, name="woven_a", align_bytes=64)
+        nc.vector.tensor_copy(*views(woven_b, raw_b, 0, 88))
+        nc.scalar.copy(*views(woven_b, raw_b, 88, Q))
+
+        def quantise(woven, name):
+            codes = sb.tile([P, Q], U32, name=name + "_codes", tag=name + "_codes", align_bytes=64)
+            scales = sb.tile([P, Q], U8, name=name + "_scales", align_bytes=64)
+            nc.vector.quantize_mx(codes[:].bitcast(FP8X4), scales[:], woven[:].rearrange("p q j -> p (q j)"))
+            return codes, scales
+
+        def score(quantised, lo, hi, name):
+            codes, scales = quantised
+            bank = ps.tile([P, hi - lo], F32, name=name)
+            nc.tensor.matmul_mx(
+                bank[:], lhsT=codes[:].bitcast(FP8X4), lhsT_scale=scales[:],
+                rhs=key_words[:, 2 * lo : 2 * hi].bitcast(FP4X4), rhs_scale=key_scales[:, lo:hi],
+                start=True, stop=True,
+            )
+            return bank
+
+        quant_b = quantise(woven_b, "qb")
+        nc.vector.tensor_copy(*views(woven_a, raw_a, 0, Q))
+        quant_a = quantise(woven_a, "qa")
+
+        b_all = sb.tile([P, T], F32, name="b_all")
+        for n in range(4):
+            lo, hi = 256 * n, 256 * (n + 1)
+            bank = score(quant_b, lo, hi, "bank_b%d" % n)
+            if n != 2:
+                nc.scalar.copy(b_all[:, lo:hi], bank[:])
+            else:
+                nc.vector.tensor_copy(b_all[:, lo:hi], bank[:])
+        a_all = sb.tile([P, T], F32, name="a_all")
+        spans_a = [(0, 256), (256, 512), (512, T)]
+        banks_a = [score(quant_a, lo, hi, "bank_a%d" % lo) for lo, hi in spans_a]
+        nc.vector.tensor_copy(a_all[:, 0:256], banks_a[0][:])
+
+        shifted_lo = sb.tile([P, HALF], F32, name="shifted_lo")
+        falling = sb.tile([P, I], F32, name="falling")
+
+        def shift(shifted, lo, hi):
+            nc.vector.tensor_scalar(shifted[:], b_all[:].indirect(list_b[:, cols(lo, hi)]), 1.0, 0.5, ALU.mult, ALU.add)
+
+        shift(shifted_lo, 0, HALF)
+        nc.scalar.activation(falling[:, HALF:], b_all[:].indirect(list_b[:, cols(HALF, I)]), ACT.Sigmoid, scale=-1.0)
+        nc.scalar.activation(falling[:, :HALF], shifted_lo[:], ACT.Sigmoid, bias=half[:], scale=-1.0)
+
+        for (lo, hi), bank in zip(spans_a[1:], banks_a[1:]):
+            nc.vector.tensor_copy(a_all[:, lo:hi], bank[:])
+        shifted_hi = sb.tile([P, HALF], F32, name="shifted_hi", tag="qa_codes", align_bytes=64)
+        shift(shifted_hi, HALF, I)
+        worth = sb.tile([P, I], F32, name="worth")
+        nc.vector.tensor_tensor(worth[:, :HALF], a_all[:].indirect(list_a[:, cols(0, HALF)]), lam_wide[:], ALU.mult)
+
+        logs = sb.tile([P, I], F32, name="logs")
+        lean = sb.tile([P, I], F32, name="lean")
+        inv = sb.tile([P, I], F32, name="inv")
+        root = sb.tile([P, I], F32, name="root")
+
+        def log_of(lo, hi):
+            nc.scalar.activation(logs[:, lo:hi], falling[:, lo:hi], ACT.Ln, bias=TINY, scale=math.exp(-0.5))
+
+        def lean_of(lo, hi, shifted):
+            nc.vector.scalar_tensor_tensor(lean[:, lo:hi], logs[:, lo:hi], -1.0, shifted, ALU.mult, ALU.max)
+
+        def root_of(lo, hi):
+            nc.scalar.activation(root[:, lo:hi], lean[:, lo:hi], ACT.Abs_reciprocal_sqrt)
+
+        def square(lo, hi):
+            nc.scalar.activation(inv[:, lo:hi], root[:, lo:hi], ACT.Square)
+
+        def place(lo, hi):
+            nc.vector.tensor_tensor(placed[:].indirect(list_a[:, cols(lo, hi)]), worth[:, lo:hi], inv[:, lo:hi], ALU.mult)
+
+        log_of(0, 128)
+        log_of(128, 256)
+        log_of(256, 512)
+        lean_of(0, 128, shifted_lo[:, :128])
+        lean_of(128, 256, shifted_lo[:, 128:])
+        nc.vector.reciprocal(inv[:, :FIRST], lean[:, :FIRST])
+        lean_of(HALF, I, shifted_hi[:])
+        place(0, 128)
+        root_of(128, 256)
+        square(128, 256)
+        place(128, 256)
+        root_of(HALF, I)
+        nc.scalar.activation(lean[:, :HALF], a_all[:].indirect(list_a[:, cols(HALF, I)]), ACT.Copy)
+        square(HALF, I)
+        nc.scalar.activation(worth[:, HALF:], lean[:, :HALF], ACT.Copy, scale=lam_col[:])
+        place(HALF, I)
+
+        summed = sb.tile([P, T], F32, name="summed")
+        nc.vector.tensor_tensor(summed[:], placed[:], totals[:], ALU.add)
+        res_v = sb.tile([P, HALF], F32, name="res_v")
+        res_s = sb.tile([P, HALF], F32, name="res_s")
+        nc.vector.tensor_copy(res_v[:], summed[:].indirect(list_o[:, cols(0, HALF)]))
+        nc.scalar.activation(res_s[:], summed[:].indirect(list_o[:, cols(HALF, I)]), ACT.Copy)
+        nc.sync.dma_start(out[:, :HALF], res_v[:])
+        nc.scalar.dma_start(out[:, HALF:], res_s[:])

@@ -40,24 +40,22 @@ def tile_attend_worthfor_lean_through_heads_kernel(tc, query, query2, keys_words
 
         key_scales = sb.tile([P, T], U8, name="key_scales", align_bytes=64)
         nc.vector.memset(key_scales[:].bitcast(I32), 0)
-        lam_col = sb.tile([P, 1], F32, name="lam_col")
-        nc.scalar.dma_start(lam_col[:], lam)
         zero = sb.tile([P, HALF], F32, name="zero")
         nc.vector.memset(zero[:], 0.0)
         half = sb.tile([P, 1], F32, name="half")
         nc.scalar.activation(half[:], zero[:, 0:1], ACT.Sigmoid)
-        lam_wide = sb.tile([P, HALF], F32, name="lam_wide")
-        nc.scalar.activation(lam_wide[:], zero[:], ACT.Identity, bias=lam_col[:])
 
         raw_b = sb.tile([P, PACK, Q], F32, name="raw_b")
         nc.sync.dma_start(raw_b[:], query2.rearrange("(p j) q -> p j q", j=PACK))
+        key_words = sb.tile([P, 2 * T], U8, name="key_words", align_bytes=64)
+        nc.sync.dma_start(key_words[:].bitcast(I32), keys_words[0].bitcast(I32))
+        lam_col = sb.tile([P, 1], F32, name="lam_col")
+        nc.sync.dma_start(lam_col[:], lam)
         for quad in range(4):
             nc.sync.dma_start(
                 key_scales[32 * quad : 32 * quad + 4, :].bitcast(I32),
                 keys_scales[0, 4 * quad : 4 * quad + 4, :].bitcast(I32),
             )
-        key_words = sb.tile([P, 2 * T], U8, name="key_words", align_bytes=64)
-        nc.sync.dma_start(key_words[:].bitcast(I32), keys_words[0].bitcast(I32))
         raw_a = sb.tile([P, PACK, Q], F32, name="raw_a")
         nc.sync.dma_start(raw_a[:], query.rearrange("(p j) q -> p j q", j=PACK))
         nc.sync.dma_start(list_b[:], offs2)
@@ -76,6 +74,8 @@ def tile_attend_worthfor_lean_through_heads_kernel(tc, query, query2, keys_words
         woven_a = sb.tile([P, Q, PACK], BF16, name="woven_a", align_bytes=64)
         nc.vector.tensor_copy(*views(woven_b, raw_b, 0, 88))
         nc.scalar.copy(*views(woven_b, raw_b, 88, Q))
+        lam_wide = sb.tile([P, HALF], F32, name="lam_wide")
+        nc.scalar.activation(lam_wide[:], zero[:], ACT.Identity, bias=lam_col[:])
 
         def quantise(woven, name):
             codes = sb.tile([P, Q], U32, name=name + "_codes", tag=name + "_codes", align_bytes=64)
@@ -98,32 +98,30 @@ def tile_attend_worthfor_lean_through_heads_kernel(tc, query, query2, keys_words
         quant_a = quantise(woven_a, "qa")
 
         b_all = sb.tile([P, T], F32, name="b_all")
-        for n in range(4):
-            lo, hi = 256 * n, 256 * (n + 1)
+        for n, (lo, hi) in enumerate([(0, 256), (256, 512), (512, 768), (768, 896), (896, T)]):
             bank = score(quant_b, lo, hi, "bank_b%d" % n)
-            if n != 2:
+            if n != 3:
                 nc.scalar.copy(b_all[:, lo:hi], bank[:])
             else:
                 nc.vector.tensor_copy(b_all[:, lo:hi], bank[:])
         a_all = sb.tile([P, T], F32, name="a_all")
         spans_a = [(0, 256), (256, 512), (512, T)]
         banks_a = [score(quant_a, lo, hi, "bank_a%d" % lo) for lo, hi in spans_a]
-        nc.vector.tensor_copy(a_all[:, 0:256], banks_a[0][:])
 
-        shifted_lo = sb.tile([P, HALF], F32, name="shifted_lo")
+        shifted_hi = sb.tile([P, HALF], F32, name="shifted_hi")
         falling = sb.tile([P, I], F32, name="falling")
 
         def shift(shifted, lo, hi):
             nc.vector.tensor_scalar(shifted[:], b_all[:].indirect(list_b[:, cols(lo, hi)]), 1.0, 0.5, ALU.mult, ALU.add)
 
-        shift(shifted_lo, 0, HALF)
-        nc.scalar.activation(falling[:, HALF:], b_all[:].indirect(list_b[:, cols(HALF, I)]), ACT.Sigmoid, scale=-1.0)
-        nc.scalar.activation(falling[:, :HALF], shifted_lo[:], ACT.Sigmoid, bias=half[:], scale=-1.0)
-
-        for (lo, hi), bank in zip(spans_a[1:], banks_a[1:]):
-            nc.vector.tensor_copy(a_all[:, lo:hi], bank[:])
-        shifted_hi = sb.tile([P, HALF], F32, name="shifted_hi", tag="qa_codes", align_bytes=64)
         shift(shifted_hi, HALF, I)
+        nc.scalar.activation(falling[:, :HALF], b_all[:].indirect(list_b[:, cols(0, HALF)]), ACT.Sigmoid, scale=-1.0)
+        nc.scalar.activation(falling[:, HALF:], shifted_hi[:], ACT.Sigmoid, bias=half[:], scale=-1.0)
+
+        for (lo, hi), bank in zip(spans_a, banks_a):
+            nc.vector.tensor_copy(a_all[:, lo:hi], bank[:])
+        shifted_lo = sb.tile([P, HALF], F32, name="shifted_lo", tag="qa_codes", align_bytes=64)
+        shift(shifted_lo, 0, HALF)
         worth = sb.tile([P, I], F32, name="worth")
         nc.vector.tensor_tensor(worth[:, :HALF], a_all[:].indirect(list_a[:, cols(0, HALF)]), lam_wide[:], ALU.mult)
 

import math
from contextlib import ExitStack

import concourse.mybir as mybir

D, T, I, Q = 512, 1024, 512, 128
FLOPS = 2 * 2 * D * T * Q

F32 = mybir.dt.float32
BF16 = mybir.dt.bfloat16
I32 = mybir.dt.int32
U32 = mybir.dt.uint32
U16 = mybir.dt.uint16
U8 = mybir.dt.uint8
FP8X4 = mybir.dt.float8_e4m3fn_x4
FP4X4 = mybir.dt.float4_e2m1fn_x4
ALU = mybir.AluOpType
ACT = mybir.ActivationFunctionType

P = 128
PACK = 4
LANES = 16
HALF = I // 2
FIRST = 128
TINY = 2.0 ** -63


def tile_attend_worthfor_lean_through_heads_kernel(tc, query, query2, keys_words, keys_scales, lam, old, offs, offs2, offs3, out):
    nc = tc.nc
    with ExitStack() as ctx:
        sb = ctx.enter_context(tc.tile_pool(name="sb", bufs=1))
        ps = ctx.enter_context(tc.psum_pool(name="ps", bufs=1))

        def cols(lo, hi):
            return slice(lo // LANES, hi // LANES)

        list_a = sb.tile([P, I // LANES], U16, name="list_a")
        list_b = sb.tile([P, I // LANES], U16, name="list_b")
        list_o = sb.tile([P, I // LANES], U16, name="list_o")

        key_scales = sb.tile([P, T], U8, name="key_scales", align_bytes=64)
        nc.vector.memset(key_scales[:].bitcast(I32), 0)
        zero = sb.tile([P, HALF], F32, name="zero")
        nc.vector.memset(zero[:], 0.0)
        half = sb.tile([P, 1], F32, name="half")
        nc.scalar.activation(half[:], zero[:, 0:1], ACT.Sigmoid)

        raw_b = sb.tile([P, PACK, Q], F32, name="raw_b")
        nc.sync.dma_start(raw_b[:], query2.rearrange("(p j) q -> p j q", j=PACK))
        key_words = sb.tile([P, 2 * T], U8, name="key_words", align_bytes=64)
        nc.sync.dma_start(key_words[:].bitcast(I32), keys_words[0].bitcast(I32))
        lam_col = sb.tile([P, 1], F32, name="lam_col")
        nc.sync.dma_start(lam_col[:], lam)
        for quad in range(4):
            nc.sync.dma_start(
                key_scales[32 * quad : 32 * quad + 4, :].bitcast(I32),
                keys_scales[0, 4 * quad : 4 * quad + 4, :].bitcast(I32),
            )
        raw_a = sb.tile([P, PACK, Q], F32, name="raw_a")
        nc.sync.dma_start(raw_a[:], query.rearrange("(p j) q -> p j q", j=PACK))
        nc.sync.dma_start(list_b[:], offs2)
        nc.sync.dma_start(list_a[:], offs)
        totals = sb.tile([P, T], F32, name="totals")
        nc.sync.dma_start(totals[:], old)
        nc.sync.dma_start(list_o[:], offs3)

        placed = sb.tile([P, T], F32, name="placed")
        nc.vector.memset(placed[:], 0.0)

        def views(woven, raw, lo, hi):
            return (woven[:, lo:hi, :].rearrange("p (c i) j -> p c j i", i=4), raw[:, :, lo:hi].rearrange("p j (c i) -> p c j i", i=4))

        woven_b = sb.tile([P, Q, PACK], BF16, name="woven_b", align_bytes=64)
        woven_a = sb.tile([P, Q, PACK], BF16, name="woven_a", align_bytes=64)
        nc.vector.tensor_copy(*views(woven_b, raw_b, 0, 88))
        nc.scalar.copy(*views(woven_b, raw_b, 88, Q))
        lam_wide = sb.tile([P, HALF], F32, name="lam_wide")
        nc.scalar.activation(lam_wide[:], zero[:], ACT.Identity, bias=lam_col[:])

        def quantise(woven, name):
            codes = sb.tile([P, Q], U32, name=name + "_codes", tag=name + "_codes", align_bytes=64)
            scales = sb.tile([P, Q], U8, name=name + "_scales", align_bytes=64)
            nc.vector.quantize_mx(codes[:].bitcast(FP8X4), scales[:], woven[:].rearrange("p q j -> p (q j)"))
            return codes, scales

        def score(quantised, lo, hi, name):
            codes, scales = quantised
            bank = ps.tile([P, hi - lo], F32, name=name)
            nc.tensor.matmul_mx(
                bank[:], lhsT=codes[:].bitcast(FP8X4), lhsT_scale=scales[:],
                rhs=key_words[:, 2 * lo : 2 * hi].bitcast(FP4X4), rhs_scale=key_scales[:, lo:hi],
                start=True, stop=True,
            )
            return bank

        quant_b = quantise(woven_b, "qb")
        nc.vector.tensor_copy(*views(woven_a, raw_a, 0, Q))
        quant_a = quantise(woven_a, "qa")

        b_all = sb.tile([P, T], F32, name="b_all")
        for n, (lo, hi) in enumerate([(0, 256), (256, 512), (512, 768), (768, 896), (896, T)]):
            bank = score(quant_b, lo, hi, "bank_b%d" % n)
            if n != 3:
                nc.scalar.copy(b_all[:, lo:hi], bank[:])
            else:
                nc.vector.tensor_copy(b_all[:, lo:hi], bank[:])
        a_all = sb.tile([P, T], F32, name="a_all")
        spans_a = [(0, 256), (256, 512), (512, T)]
        banks_a = [score(quant_a, lo, hi, "bank_a%d" % lo) for lo, hi in spans_a]

        shifted_hi = sb.tile([P, HALF], F32, name="shifted_hi")
        falling = sb.tile([P, I], F32, name="falling")

        def shift(shifted, lo, hi):
            nc.vector.tensor_scalar(shifted[:], b_all[:].indirect(list_b[:, cols(lo, hi)]), 1.0, 0.5, ALU.mult, ALU.add)

        shift(shifted_hi, HALF, I)
        nc.scalar.activation(falling[:, :HALF], b_all[:].indirect(list_b[:, cols(0, HALF)]), ACT.Sigmoid, scale=-1.0)
        nc.scalar.activation(falling[:, HALF:], shifted_hi[:], ACT.Sigmoid, bias=half[:], scale=-1.0)

        for (lo, hi), bank in zip(spans_a, banks_a):
            nc.vector.tensor_copy(a_all[:, lo:hi], bank[:])
        shifted_lo = sb.tile([P, HALF], F32, name="shifted_lo", tag="qa_codes", align_bytes=64)
        shift(shifted_lo, 0, HALF)
        worth = sb.tile([P, I], F32, name="worth")
        nc.vector.tensor_tensor(worth[:, :HALF], a_all[:].indirect(list_a[:, cols(0, HALF)]), lam_wide[:], ALU.mult)

        logs = sb.tile([P, I], F32, name="logs")
        lean = sb.tile([P, I], F32, name="lean")
        inv = sb.tile([P, I], F32, name="inv")
        root = sb.tile([P, I], F32, name="root")

        def log_of(lo, hi):
            nc.scalar.activation(logs[:, lo:hi], falling[:, lo:hi], ACT.Ln, bias=TINY, scale=math.exp(-0.5))

        def lean_of(lo, hi, shifted):
            nc.vector.scalar_tensor_tensor(lean[:, lo:hi], logs[:, lo:hi], -1.0, shifted, ALU.mult, ALU.max)

        def root_of(lo, hi):
            nc.scalar.activation(root[:, lo:hi], lean[:, lo:hi], ACT.Abs_reciprocal_sqrt)

        def square(lo, hi):
            nc.scalar.activation(inv[:, lo:hi], root[:, lo:hi], ACT.Square)

        def place(lo, hi):
            nc.vector.tensor_tensor(placed[:].indirect(list_a[:, cols(lo, hi)]), worth[:, lo:hi], inv[:, lo:hi], ALU.mult)

        log_of(0, 128)
        log_of(128, 256)
        log_of(256, 512)
        lean_of(0, 128, shifted_lo[:, :128])
        lean_of(128, 256, shifted_lo[:, 128:])
        nc.vector.reciprocal(inv[:, :FIRST], lean[:, :FIRST])
        lean_of(HALF, I, shifted_hi[:])
        place(0, 128)
        root_of(128, 256)
        square(128, 256)
        place(128, 256)
        root_of(HALF, I)
        nc.scalar.activation(lean[:, :HALF], a_all[:].indirect(list_a[:, cols(HALF, I)]), ACT.Copy)
        square(HALF, I)
        nc.scalar.activation(worth[:, HALF:], lean[:, :HALF], ACT.Copy, scale=lam_col[:])
        place(HALF, I)

        summed = sb.tile([P, T], F32, name="summed")
        nc.vector.tensor_tensor(summed[:], placed[:], totals[:], ALU.add)
        res_v = sb.tile([P, HALF], F32, name="res_v")
        res_s = sb.tile([P, HALF], F32, name="res_s")
        nc.vector.tensor_copy(res_v[:], summed[:].indirect(list_o[:, cols(0, HALF)]))
        nc.scalar.activation(res_s[:], summed[:].indirect(list_o[:, cols(HALF, I)]), ACT.Copy)
        nc.sync.dma_start(out[:, :HALF], res_v[:])
        nc.scalar.dma_start(out[:, HALF:], res_s[:])
